import numpy as np
import ml_dtypes


def mxq(x, axis, fmt="e4m3"):
    dtype, down = {"e4m3": (ml_dtypes.float8_e4m3fn, 7), "e5m2": (ml_dtypes.float8_e5m2, 14)}[fmt]
    v = np.moveaxis(np.asarray(x, np.float32).astype(ml_dtypes.bfloat16).astype(np.float64), axis, -1)
    blocks = v.reshape(v.shape[:-1] + (-1, 32))
    amax = np.abs(blocks).max(-1, keepdims=True)
    byte = np.maximum(np.where(amax > 0, np.frexp(amax)[1] - 1 + 127, 0) - down, 1)
    scale = np.exp2(byte - 127.0)
    codes = (blocks / scale).astype(np.float32).astype(dtype).astype(np.float64)
    return np.moveaxis((codes * scale).reshape(v.shape), -1, axis)


WIDE = False


def mx_kscale(k):
    if not WIDE:
        return np.ones(k)
    levels = np.array([10, -10, 5, -5, 0])
    if k % 512:
        return np.exp2(np.random.permutation(np.resize(levels, k // 32))).repeat(32)
    a = np.empty((k // 512, 16))
    for p in range(k // 512):
        a[p, :8] = np.random.permutation(np.resize(levels, 8))
        for g in range(8):
            far = levels[np.abs(levels - a[p, g]) >= 10]
            a[p, g + 8] = far[np.random.randint(len(far))]
    return np.exp2(a.ravel()).repeat(32)


def f64(x):
    return np.asarray(x).astype(np.float64)


def striped(idx):
    return np.tile(idx.reshape(-1, 16).T, (8, 1)).astype(np.uint16)


def unstriped(offs):
    return offs[:16].T.reshape(-1).astype(np.int64)


E2M1 = np.array([0.0, 0.5, 1.0, 1.5, 2.0, 3.0, 4.0, 6.0, -0.0, -0.5, -1.0, -1.5, -2.0, -3.0, -4.0, -6.0])


def pack_weight(w, fmt):
    k, n = w.shape
    w = f64(np.asarray(w, np.float32).astype(ml_dtypes.bfloat16)).reshape(k // 32, 32, n)
    amax = np.abs(w).max(1)
    if fmt == "e4m3":
        byte = np.frexp(amax)[1] - 1 + 127 - 7
    else:
        mant, ex = np.frexp(amax / 6.0)
        byte = np.where(mant > 0.5, ex, ex - 1) + 127
    byte = np.clip(np.where(amax > 0, byte, 1), 1, 254)
    scaled = (w * np.exp2(127.0 - byte)[:, None, :]).reshape(k, n).astype(np.float32)
    by_word = np.ascontiguousarray(scaled.reshape(k // 512, 128, 4, n).transpose(0, 1, 3, 2))
    if fmt == "e4m3":
        words = by_word.astype(ml_dtypes.float8_e4m3fn).view(np.uint8)
    else:
        c = by_word.astype(ml_dtypes.float4_e2m1fn).view(np.uint8) & 0xF
        words = (c[..., 0::2] | (c[..., 1::2] << 4)).reshape(k // 512, 128, 2 * n)
    return np.ascontiguousarray(words), np.ascontiguousarray(byte.astype(np.uint8).reshape(k // 512, 16, n))


def unpack_weight(words, scales, fmt):
    g, _, n = scales.shape
    words = np.ascontiguousarray(words).reshape(g, 128, n, -1)
    if fmt == "e4m3":
        vals = words.view(ml_dtypes.float8_e4m3fn).astype(np.float64)
    else:
        nib = np.empty((g, 128, n, 4), np.uint8)
        nib[..., 0::2] = words & 0xF
        nib[..., 1::2] = words >> 4
        vals = E2M1[nib]
    vals = vals * np.repeat(np.exp2(scales.astype(np.float64) - 127.0), 8, axis=1)[..., None]
    return vals.transpose(0, 1, 3, 2).reshape(g * 512, n)


def gelu(v):
    return 0.5 * v * (1.0 + np.tanh(np.sqrt(2.0 / np.pi) * (v + 0.044715 * v**3)))


K, H, N, T, S, P = 1536, 512, 768, 4096, 1024, 512

def setup_inputs():
    n = np.random.standard_normal
    s = mx_kscale(K)[:, None]
    u = mx_kscale(H)[:, None]
    tab_words, tab_scales = pack_weight(n((K, T)) * s, "e4m3")
    w4_words, w4_scales = pack_weight(1.2 * n((K, H)) / np.sqrt(K) / s, "e2m1")
    w8_words, w8_scales = pack_weight(n((H, N)) / np.sqrt(H) / u, "e4m3")
    perm = np.random.permutation(S)
    return {
        "tab_words": tab_words, "tab_scales": tab_scales,
        "offs": striped(np.random.permutation(T)[:S]),
        "pos1": striped(perm[:P]),
        "pos2": striped(perm[P:]),
        "w1": (0.5 * n((K, H)) / np.sqrt(K) / s).astype(np.float32),
        "w4_words": w4_words, "w4_scales": w4_scales,
        "b4": (0.5 * n(H)).astype(np.float32),
        "sharp": np.random.uniform(1, 3, H).astype(np.float32),
        "share": np.random.uniform(0.1, 0.5, H).astype(np.float32),
        "pat": (2.0 * n((H, P))).astype(np.float32),
        "skip": np.random.uniform(0.5, 1.5, H).astype(np.float32),
        "wgs": np.exp(0.3 * n((128, P))).astype(np.float32),
        "gain": (np.random.uniform(0.5, 2.0, H) * u[:, 0]).astype(np.float32),
        "w8_words": w8_words, "w8_scales": w8_scales,
    }

def reference(tab_words, tab_scales, offs, pos1, pos2, w1, w4_words, w4_scales, b4, sharp, share, pat, skip, wgs, gain, w8_words, w8_scales):
    v = unpack_weight(tab_words, tab_scales, "e4m3")[:, unstriped(offs)]
    w1q = mxq(f64(w1), 0, "e4m3")
    w4 = unpack_weight(w4_words, w4_scales, "e2m1")
    w8 = unpack_weight(w8_words, w8_scales, "e4m3")
    h = (w1q.T @ v) + np.tanh((w4.T @ v) + f64(b4)[:, None])
    top = h.max(axis=1)
    a = 1.0 / (1.0 + np.exp(-f64(sharp)[:, None] * (h[:, unstriped(pos1)] - f64(share)[:, None] * top[:, None])))
    a = a * f64(pat)
    page = f64(skip)[:, None] * h
    page[:, unstriped(pos2)] = np.tile(f64(wgs), (H // 128, 1)) * a
    x = mxq(page * f64(gain)[:, None], 0, "e4m3")
    return w8.T @ x

@@ -1,0 +1,248 @@
+from contextlib import ExitStack
+
+import concourse.mybir as mybir
+
+K, H, N, T, S, PICK = 1536, 512, 768, 4096, 1024, 512
+FLOPS = 2 * (2 * K * H * S + H * N * S)
+
+F32 = mybir.dt.float32
+BF16 = mybir.dt.bfloat16
+I32 = mybir.dt.int32
+U32 = mybir.dt.uint32
+U16 = mybir.dt.uint16
+U8 = mybir.dt.uint8
+FP8X4 = mybir.dt.float8_e4m3fn_x4
+FP4X4 = mybir.dt.float4_e2m1fn_x4
+ACT = mybir.ActivationFunctionType
+ALU = mybir.AluOpType
+
+P = 128
+PACK = 4
+PASSES = K // (P * PACK)
+BANK = 512
+HALVES = S // BANK
+QUADS = 4
+SHIFT_ROWS = 112
+
+
+def tile_list_crackle_patch_readout_kernel(
+    tc, tab_words, tab_scales, offs, pos1, pos2, w1, w4_words, w4_scales, b4, sharp, share, pat, skip, wgs, gain,
+    w8_words, w8_scales, out,
+):
+    nc = tc.nc
+    with ExitStack() as ctx:
+        lists = ctx.enter_context(tc.tile_pool(name="lists", bufs=1))
+        keep = ctx.enter_context(tc.tile_pool(name="keep", bufs=1))
+        ring = ctx.enter_context(tc.tile_pool(name="ring", bufs=2))
+        psum = ctx.enter_context(tc.psum_pool(name="psum", bufs=1))
+
+        def half(h):
+            return slice(h * BANK, (h + 1) * BANK)
+
+        tab_sc = keep.tile([P, T], U8, name="tab_sc", align_bytes=64)
+        nc.vector.memset(tab_sc[:].bitcast(I32), 0)
+        w4_sc_raw = keep.tile([P, PASSES, H], U8, name="w4_sc_raw", align_bytes=64)
+        nc.vector.memset(w4_sc_raw[:].rearrange("p a n -> p (a n)").bitcast(I32), 0)
+        v_sc = [keep.tile([P, S], U8, name=f"v_sc{a}", align_bytes=64) for a in range(PASSES)]
+        for a in range(1, PASSES):
+            nc.gpsimd.memset(v_sc[a][:].bitcast(I32), 0)
+        w8_sc = keep.tile([P, N], U8, name="w8_sc", align_bytes=64)
+        nc.gpsimd.memset(w8_sc[:].bitcast(I32), 0)
+
+        offs_sb = lists.tile([P, S // 16], U16, name="offs_sb")
+        pos1_sb = lists.tile([P, PICK // 16], U16, name="pos1_sb")
+        pos2_sb = lists.tile([P, PICK // 16], U16, name="pos2_sb")
+        tab_sb = [keep.tile([P, T], I32, name=f"tab{a}", align_bytes=64) for a in range(PASSES)]
+        w1_raw = [keep.tile([P, PACK, H], F32, name=f"w1_raw{a}") for a in range(PASSES)]
+        w4_raw = keep.tile([P, PASSES, H // 2], I32, name="w4_raw")
+        nc.sync.dma_start(offs_sb[:], offs)
+        for a in range(PASSES):
+            nc.sync.dma_start(tab_sb[a][:], tab_words[a].rearrange("p t i -> p (t i)").bitcast(I32))
+            if a == 0:
+                nc.sync.dma_start(w4_raw[:], w4_words.rearrange("a p n -> p a n").bitcast(I32))
+            nc.sync.dma_start(
+                w1_raw[a][:], w1[a * P * PACK : (a + 1) * P * PACK, :].rearrange("(p j) c -> p j c", j=PACK)
+            )
+        nc.sync.dma_start(pos1_sb[:], pos1)
+        nc.sync.dma_start(pos2_sb[:], pos2)
+        wgs_sb = keep.tile([P, PACK * PICK], F32, name="wgs_sb")
+        for q in range(QUADS):
+            nc.sync.dma_start(wgs_sb[32 * q : 32 * (q + 1), :], wgs.rearrange("(p t) m -> p (t m)", t=PACK))
+        pat_rows = pat.rearrange("(p t) m -> p t m", t=PACK)
+        pat_sb = [keep.tile([P, 2, PICK], F32, name=f"pat{u}") for u in range(2)]
+        for u in (1, 0):
+            nc.sync.dma_start(pat_sb[u][:], pat_rows[:, 2 * u : 2 * u + 2, :])
+        w8_sb = keep.tile([P, N], I32, name="w8_sb", align_bytes=64)
+        nc.sync.dma_start(w8_sb[:], w8_words[0].rearrange("p n i -> p (n i)").bitcast(I32))
+
+        for q in range(QUADS):
+            nc.gpsimd.dma_start(
+                tab_sc[32 * q : 32 * q + 4 * PASSES, :].bitcast(I32), tab_scales[:, 4 * q : 4 * q + 4, :].bitcast(I32)
+            )
+        for q in range(QUADS):
+            nc.gpsimd.dma_start(
+                w4_sc_raw[32 * q : 32 * q + 4, :, :].bitcast(I32),
+                w4_scales[:, 4 * q : 4 * q + 4, :].rearrange("a r n -> r a n").bitcast(I32),
+            )
+
+        nc.vector.tensor_copy(v_sc[0][:], tab_sc[:].indirect(offs_sb[:]))
+        for a in range(1, PASSES):
+            nc.gpsimd.dma_start(
+                v_sc[a][0:SHIFT_ROWS, :].bitcast(I32), v_sc[0][4 * a : 4 * a + SHIFT_ROWS, :].bitcast(I32)
+            )
+
+        row_vals = {}
+        for name, vec in (("b4", b4), ("sharp", sharp), ("share", share), ("skip", skip), ("gain", gain)):
+            row_vals[name] = keep.tile([P, PACK], F32, name=f"{name}_sb")
+            nc.scalar.dma_start(row_vals[name][:], vec.rearrange("(p t) -> p t", t=PACK))
+        for q in range(QUADS):
+            nc.gpsimd.dma_start(
+                w8_sc[32 * q : 32 * q + 4, :].bitcast(I32), w8_scales[0, 4 * q : 4 * q + 4, :].bitcast(I32)
+            )
+
+        w4_sb = keep.tile([P, PASSES, 2 * H], U8, name="w4_sb", align_bytes=64)
+        w4_sc = keep.tile([P, PASSES, H], U8, name="w4_sc", align_bytes=64)
+        nc.vector.tensor_copy(
+            w4_sb[:].bitcast(U16).rearrange("p a (t m) -> p a m t", t=PACK),
+            w4_raw[:].bitcast(U16).rearrange("p a (m t) -> p a m t", t=PACK),
+        )
+        nc.vector.tensor_copy(
+            w4_sc[:].rearrange("p a (t m) -> p a m t", t=PACK),
+            w4_sc_raw[:].rearrange("p a (m t) -> p a m t", t=PACK),
+        )
+        neg_open = keep.tile([P, PACK], F32, name="neg_open")
+        opening = keep.tile([P, PACK], F32, name="opening")
+        nc.gpsimd.tensor_tensor(opening[:], row_vals["sharp"][:], row_vals["share"][:], ALU.mult)
+        nc.gpsimd.tensor_scalar(neg_open[:], opening[:], -1.0, 0.0, ALU.mult, ALU.add)
+
+        v_words = [[keep.tile([P, BANK], U32, name=f"v{a}_{h}", align_bytes=64) for h in range(HALVES)] for a in range(PASSES)]
+        w1_q = [keep.tile([P, H], U32, name=f"w1_q{a}", align_bytes=64) for a in range(PASSES)]
+        w1_sc = [keep.tile([P, H], U8, name=f"w1_sc{a}", align_bytes=64) for a in range(PASSES)]
+
+        def gather_pass(a):
+            cols = BANK // 16
+            for h in range(HALVES):
+                nc.vector.tensor_copy(
+                    v_words[a][h][:], tab_sb[a][:].bitcast(U32).indirect(offs_sb[:, h * cols : (h + 1) * cols])
+                )
+
+        def quantise_w1(a):
+            grouped = ring.tile([P, H * PACK], BF16, name="w1_grouped", align_bytes=64)
+            dst = grouped[:].rearrange("p (t m j) -> p m j t", t=PACK, j=PACK)
+            src = w1_raw[a][:].rearrange("p j (m t) -> p m j t", t=PACK)
+            if a < PASSES - 1:
+                nc.scalar.copy(dst, src)
+            else:
+                nc.vector.tensor_copy(dst, src)
+            nc.vector.quantize_mx(w1_q[a][:].bitcast(FP8X4), w1_sc[a][:], grouped[:])
+
+        sums = {}
+
+        def first_stage_pass(t, a, kinds):
+            m = slice(t * P, (t + 1) * P)
+            for kind in kinds:
+                for h in range(HALVES):
+                    if a == 0:
+                        bank = 4 * (t % 2) + 2 * (kind == "w1") + h
+                        sums[t, kind, h] = psum.tile([P, BANK], F32, name=f"bank{bank}")
+                    if kind == "w4":
+                        lhs = w4_sb[:, a, 2 * t * P : 2 * (t + 1) * P].bitcast(FP4X4)
+                        lhs_sc = w4_sc[:, a, m]
+                    else:
+                        lhs = w1_q[a][:, m].bitcast(FP8X4)
+                        lhs_sc = w1_sc[a][:, m]
+                    nc.tensor.matmul_mx(
+                        sums[t, kind, h][:], lhsT=lhs, lhsT_scale=lhs_sc,
+                        rhs=v_words[a][h][:].bitcast(FP8X4), rhs_scale=v_sc[a][:, half(h)],
+                        start=(a == 0), stop=(a == PASSES - 1),
+                    )
+
+        for a in range(PASSES):
+            gather_pass(a)
+            quantise_w1(a)
+            for kind in ("w4", "w1"):
+                for t in range(2):
+                    first_stage_pass(t, a, (kind,))
+
+        pw, bounded = {}, {}
+
+        def bound(t):
+            for h in range(HALVES):
+                bounded[t, h] = keep.tile([P, BANK], F32, name=f"bounded{t}_{h}")
+                nc.scalar.activation(
+                    bounded[t, h][:], sums[t, "w4", h][:], ACT.Tanh, bias=row_vals["b4"][:, t : t + 1]
+                )
+
+        def patch_weights(t):
+            pw[t] = keep.tile([P, PICK], F32, name=f"bounded{(t + 1) % PACK}_0")
+            nc.gpsimd.tensor_tensor(pw[t][:], pat_sb[t // 2][:, t % 2, :], wgs_sb[:, t * PICK : (t + 1) * PICK], ALU.mult)
+
+        top = keep.tile([P, PACK], F32, name="top")
+        look_bias = keep.tile([P, PACK], F32, name="look_bias")
+        x_rows = [keep.tile([P, PACK, BANK], BF16, name=f"x_rows{h}") for h in range(HALVES)]
+        pages, looks = {}, {}
+
+        def features(t):
+            col = slice(t, t + 1)
+            hrow = keep.tile([P, S], F32, name=f"h{t}")
+            for h in range(HALVES):
+                nc.vector.tensor_tensor(hrow[:, half(h)], sums[t, "w1", h][:], bounded[t, h][:], ALU.add)
+            patch_weights((t - 1) % PACK)
+            pages[t] = keep.tile([P, S], F32, name=f"page{t}")
+            nc.scalar.activation(pages[t][:], hrow[:], ACT.Copy, scale=row_vals["skip"][:, col])
+            nc.vector.reduce_max(top[:, col], hrow[:], axis=mybir.AxisListType.X)
+            if t == 0:
+                nc.vector.tensor_tensor(look_bias[:, col], top[:, col], neg_open[:, col], ALU.mult)
+            else:
+                nc.scalar.activation(look_bias[:, col], top[:, col], ACT.Copy, scale=neg_open[:, col])
+            looks[t] = ring.tile([P, PICK], F32, name="look")
+            nc.scalar.activation(
+                looks[t][:], hrow[:].indirect(pos1_sb[:]), ACT.Sigmoid,
+                bias=look_bias[:, col], scale=row_vals["sharp"][:, col],
+            )
+
+        def patch(t):
+            nc.vector.tensor_tensor(pages[t][:].indirect(pos2_sb[:]), looks[t][:], pw[t][:], ALU.mult)
+            for h in range(HALVES):
+                nc.scalar.activation(
+                    x_rows[h][:, t, :], pages[t][:, half(h)], ACT.Copy, scale=row_vals["gain"][:, t : t + 1]
+                )
+
+        for t in range(PACK):
+            if t >= 2:
+                for a in range(PASSES):
+                    first_stage_pass(t, a, ("w4",))
+            bound(t)
+        for t in range(PACK + 1):
+            if t < PACK:
+                if t >= 2:
+                    for a in range(PASSES):
+                        first_stage_pass(t, a, ("w1",))
+                features(t)
+            if t >= 1:
+                patch(t - 1)
+
+        n_tiles = N // P
+        for h in range(HALVES):
+            grouped = ring.tile([P, BANK * PACK], BF16, name="x_grouped", align_bytes=64)
+            nc.vector.tensor_copy(
+                grouped[:].rearrange("p (c i t) -> p c t i", i=4, t=PACK),
+                x_rows[h][:].rearrange("p t (c i) -> p c t i", i=4),
+            )
+            x_q = keep.tile([P, BANK], U32, name=f"x_q{h}", align_bytes=64)
+            x_sc = keep.tile([P, BANK], U8, name=f"x_sc{h}", align_bytes=64)
+            nc.vector.quantize_mx(x_q[:].bitcast(FP8X4), x_sc[:], grouped[:])
+            for n in range(n_tiles):
+                unit = h * n_tiles + n
+                acc = psum.tile([P, BANK], F32, name=f"bank{unit % 8}")
+                cols = slice(n * P, (n + 1) * P)
+                nc.tensor.matmul_mx(
+                    acc[:], lhsT=w8_sb[:, cols].bitcast(FP8X4), lhsT_scale=w8_sc[:, cols],
+                    rhs=x_q[:].bitcast(FP8X4), rhs_scale=x_sc[:], start=True, stop=True,
+                )
+                staged = keep.tile([P, BANK], F32, name=f"staged{unit % 8}")
+                if h == 0 or n % 3 == 2:
+                    nc.scalar.copy(staged[:], acc[:])
+                else:
+                    nc.vector.tensor_copy(staged[:], acc[:])
+                nc.sync.dma_start(out[cols, half(h)], staged[:])

@@ -22,7 +22,7 @@ PASSES = K // (P * PACK)
 BANK = 512
 HALVES = S // BANK
 QUADS = 4
-SHIFT_ROWS = 112
+CHUNK = 256
 
 
 def tile_list_crackle_patch_readout_kernel(
@@ -43,73 +43,52 @@ def tile_list_crackle_patch_readout_kernel(
         nc.vector.memset(tab_sc[:].bitcast(I32), 0)
         w4_sc_raw = keep.tile([P, PASSES, H], U8, name="w4_sc_raw", align_bytes=64)
         nc.vector.memset(w4_sc_raw[:].rearrange("p a n -> p (a n)").bitcast(I32), 0)
-        v_sc = [keep.tile([P, S], U8, name=f"v_sc{a}", align_bytes=64) for a in range(PASSES)]
-        for a in range(1, PASSES):
-            nc.gpsimd.memset(v_sc[a][:].bitcast(I32), 0)
+        v_sc = keep.tile([P, PASSES * S], U8, name="v_sc", align_bytes=64)
+        nc.vector.memset(v_sc[:].bitcast(I32), 0)
         w8_sc = keep.tile([P, N], U8, name="w8_sc", align_bytes=64)
-        nc.gpsimd.memset(w8_sc[:].bitcast(I32), 0)
+        nc.vector.memset(w8_sc[:].bitcast(I32), 0)
 
         offs_sb = lists.tile([P, S // 16], U16, name="offs_sb")
         pos1_sb = lists.tile([P, PICK // 16], U16, name="pos1_sb")
         pos2_sb = lists.tile([P, PICK // 16], U16, name="pos2_sb")
-        tab_sb = [keep.tile([P, T], I32, name=f"tab{a}", align_bytes=64) for a in range(PASSES)]
-        w1_raw = [keep.tile([P, PACK, H], F32, name=f"w1_raw{a}") for a in range(PASSES)]
-        w4_raw = keep.tile([P, PASSES, H // 2], I32, name="w4_raw")
-        nc.sync.dma_start(offs_sb[:], offs)
-        for a in range(PASSES):
+        tab_sb, w1_raw = {}, {}
+
+        def load_tab(a):
+            tab_sb[a] = keep.tile([P, T], I32, name=("tab_sc" if a == PASSES - 1 else f"tab{a}"), align_bytes=64)
             nc.sync.dma_start(tab_sb[a][:], tab_words[a].rearrange("p t i -> p (t i)").bitcast(I32))
-            if a == 0:
-                nc.sync.dma_start(w4_raw[:], w4_words.rearrange("a p n -> p a n").bitcast(I32))
+
+        def load_w1(a):
+            w1_raw[a] = keep.tile([P, PACK, H], F32, name=f"rows{a % 2}")
             nc.sync.dma_start(
                 w1_raw[a][:], w1[a * P * PACK : (a + 1) * P * PACK, :].rearrange("(p j) c -> p j c", j=PACK)
             )
+
+        w4_raw = keep.tile([P, PASSES, H // 2], I32, name="rows1")
+        nc.sync.dma_start(offs_sb[:], offs)
+        load_tab(0)
         nc.sync.dma_start(pos1_sb[:], pos1)
         nc.sync.dma_start(pos2_sb[:], pos2)
-        wgs_sb = keep.tile([P, PACK * PICK], F32, name="wgs_sb")
+        nc.sync.dma_start(w4_raw[:], w4_words.rearrange("a p n -> p a n").bitcast(I32))
+        nc.sync.dma_start(
+            tab_sc[0 : 16 * PASSES, :].bitcast(I32), tab_scales.rearrange("a q n -> q a n").bitcast(I32)
+        )
+        load_w1(0)
+        load_tab(1)
         for q in range(QUADS):
-            nc.sync.dma_start(wgs_sb[32 * q : 32 * (q + 1), :], wgs.rearrange("(p t) m -> p (t m)", t=PACK))
-        pat_rows = pat.rearrange("(p t) m -> p t m", t=PACK)
-        pat_sb = [keep.tile([P, 2, PICK], F32, name=f"pat{u}") for u in range(2)]
-        for u in (1, 0):
-            nc.sync.dma_start(pat_sb[u][:], pat_rows[:, 2 * u : 2 * u + 2, :])
-        w8_sb = keep.tile([P, N], I32, name="w8_sb", align_bytes=64)
-        nc.sync.dma_start(w8_sb[:], w8_words[0].rearrange("p n i -> p (n i)").bitcast(I32))
-
-        for q in range(QUADS):
-            nc.gpsimd.dma_start(
-                tab_sc[32 * q : 32 * q + 4 * PASSES, :].bitcast(I32), tab_scales[:, 4 * q : 4 * q + 4, :].bitcast(I32)
-            )
-        for q in range(QUADS):
-            nc.gpsimd.dma_start(
+            nc.sync.dma_start(
                 w4_sc_raw[32 * q : 32 * q + 4, :, :].bitcast(I32),
                 w4_scales[:, 4 * q : 4 * q + 4, :].rearrange("a r n -> r a n").bitcast(I32),
-            )
-
-        nc.vector.tensor_copy(v_sc[0][:], tab_sc[:].indirect(offs_sb[:]))
-        for a in range(1, PASSES):
-            nc.gpsimd.dma_start(
-                v_sc[a][0:SHIFT_ROWS, :].bitcast(I32), v_sc[0][4 * a : 4 * a + SHIFT_ROWS, :].bitcast(I32)
             )
 
         row_vals = {}
         for name, vec in (("b4", b4), ("sharp", sharp), ("share", share), ("skip", skip), ("gain", gain)):
             row_vals[name] = keep.tile([P, PACK], F32, name=f"{name}_sb")
-            nc.scalar.dma_start(row_vals[name][:], vec.rearrange("(p t) -> p t", t=PACK))
+            nc.gpsimd.dma_start(row_vals[name][:], vec.rearrange("(p t) -> p t", t=PACK))
         for q in range(QUADS):
             nc.gpsimd.dma_start(
                 w8_sc[32 * q : 32 * q + 4, :].bitcast(I32), w8_scales[0, 4 * q : 4 * q + 4, :].bitcast(I32)
             )
 
-        w4_sb = keep.tile([P, PASSES, 2 * H], U8, name="w4_sb", align_bytes=64)
-        w4_sc = keep.tile([P, PASSES, H], U8, name="w4_sc", align_bytes=64)
-        nc.vector.tensor_copy(
-            w4_sb[:].bitcast(U16).rearrange("p a (t m) -> p a m t", t=PACK),
-            w4_raw[:].bitcast(U16).rearrange("p a (m t) -> p a m t", t=PACK),
-        )
-        nc.vector.tensor_copy(
-            w4_sc[:].rearrange("p a (t m) -> p a m t", t=PACK),
-            w4_sc_raw[:].rearrange("p a (m t) -> p a m t", t=PACK),
-        )
         neg_open = keep.tile([P, PACK], F32, name="neg_open")
         opening = keep.tile([P, PACK], F32, name="opening")
         nc.gpsimd.tensor_tensor(opening[:], row_vals["sharp"][:], row_vals["share"][:], ALU.mult)
@@ -127,21 +106,18 @@ def tile_list_crackle_patch_readout_kernel(
                 )
 
         def quantise_w1(a):
-            grouped = ring.tile([P, H * PACK], BF16, name="w1_grouped", align_bytes=64)
+            grouped = keep.tile([P, H * PACK], BF16, name=f"grouped{a % 2}", align_bytes=64)
             dst = grouped[:].rearrange("p (t m j) -> p m j t", t=PACK, j=PACK)
             src = w1_raw[a][:].rearrange("p j (m t) -> p m j t", t=PACK)
-            if a < PASSES - 1:
-                nc.scalar.copy(dst, src)
-            else:
-                nc.vector.tensor_copy(dst, src)
+            nc.scalar.copy(dst, src)
             nc.vector.quantize_mx(w1_q[a][:].bitcast(FP8X4), w1_sc[a][:], grouped[:])
 
         sums = {}
 
-        def first_stage_pass(t, a, kinds):
+        def first_stage_pass(t, a, kinds, halves):
             m = slice(t * P, (t + 1) * P)
             for kind in kinds:
-                for h in range(HALVES):
+                for h in halves:
                     if a == 0:
                         bank = 4 * (t % 2) + 2 * (kind == "w1") + h
                         sums[t, kind, h] = psum.tile([P, BANK], F32, name=f"bank{bank}")
@@ -153,16 +129,49 @@ def tile_list_crackle_patch_readout_kernel(
                         lhs_sc = w1_sc[a][:, m]
                     nc.tensor.matmul_mx(
                         sums[t, kind, h][:], lhsT=lhs, lhsT_scale=lhs_sc,
-                        rhs=v_words[a][h][:].bitcast(FP8X4), rhs_scale=v_sc[a][:, half(h)],
+                        rhs=v_words[a][h][:].bitcast(FP8X4), rhs_scale=v_sc[:, a * S + h * BANK : a * S + (h + 1) * BANK],
                         start=(a == 0), stop=(a == PASSES - 1),
                     )
 
-        for a in range(PASSES):
-            gather_pass(a)
-            quantise_w1(a)
-            for kind in ("w4", "w1"):
-                for t in range(2):
-                    first_stage_pass(t, a, (kind,))
+        gather_pass(0)
+        w4_sb = keep.tile([P, PASSES, 2 * H], U8, name="w4_sb", align_bytes=64)
+        w4_sc = keep.tile([P, PASSES, H], U8, name="w4_sc", align_bytes=64)
+        nc.vector.tensor_copy(
+            w4_sb[:].bitcast(U16).rearrange("p a (t m) -> p a m t", t=PACK),
+            w4_raw[:].bitcast(U16).rearrange("p a (m t) -> p a m t", t=PACK),
+        )
+        load_w1(1)
+        quantise_w1(0)
+        load_w1(2)
+        picked_sc = keep.tile([P, S], U8, name="picked_sc", align_bytes=64)
+        nc.vector.tensor_copy(picked_sc[:], tab_sc[:].indirect(offs_sb[:]))
+        rows = 4 * PASSES
+        for q in range(QUADS):
+            nc.sync.dma_start(
+                v_sc[32 * q : 32 * q + 4, :].bitcast(I32), picked_sc[rows * q : rows * (q + 1), :].bitcast(I32)
+            )
+        load_tab(2)
+        gather_pass(1)
+        nc.vector.tensor_copy(
+            w4_sc[:].rearrange("p a (t m) -> p a m t", t=PACK),
+            w4_sc_raw[:].rearrange("p a (m t) -> p a m t", t=PACK),
+        )
+        quantise_w1(1)
+        quantise_w1(2)
+        pat_sb = keep.tile([P, PACK, PICK], F32, name="rows0")
+        nc.sync.dma_start(pat_sb[:], pat.rearrange("(p t) m -> p t m", t=PACK))
+        wgs_sb = keep.tile([P, PACK, PICK], F32, name="grouped0", align_bytes=64)
+        for q in range(QUADS):
+            nc.sync.dma_start(wgs_sb[32 * q : 32 * (q + 1), :, :], wgs.rearrange("(p t) m -> p t m", t=PACK))
+        gather_pass(2)
+        w8_sb = keep.tile([P, N], I32, name="tab_sc", align_bytes=64)
+        nc.sync.dma_start(w8_sb[:], w8_words[0].rearrange("p n i -> p (n i)").bitcast(I32))
+        for kind, a in (("w1", 0), ("w4", 0), ("w4", 1), ("w1", 1)):
+            for t in range(2):
+                first_stage_pass(t, a, (kind,), range(HALVES))
+        for h in range(HALVES):
+            for t in range(2):
+                first_stage_pass(t, PASSES - 1, ("w4", "w1"), (h,))
 
         pw, bounded = {}, {}
 
@@ -174,75 +183,91 @@ def tile_list_crackle_patch_readout_kernel(
                 )
 
         def patch_weights(t):
-            pw[t] = keep.tile([P, PICK], F32, name=f"bounded{(t + 1) % PACK}_0")
-            nc.gpsimd.tensor_tensor(pw[t][:], pat_sb[t // 2][:, t % 2, :], wgs_sb[:, t * PICK : (t + 1) * PICK], ALU.mult)
+            pw[t] = keep.tile([P, PICK], F32, name=f"pw{t}")
+            nc.gpsimd.tensor_tensor(pw[t][:], pat_sb[:, t, :], wgs_sb[:, t, :], ALU.mult)
 
         top = keep.tile([P, PACK], F32, name="top")
         look_bias = keep.tile([P, PACK], F32, name="look_bias")
-        x_rows = [keep.tile([P, PACK, BANK], BF16, name=f"x_rows{h}") for h in range(HALVES)]
-        pages, looks = {}, {}
+        pages, looks, feats = {}, {}, {}
 
         def features(t):
             col = slice(t, t + 1)
             hrow = keep.tile([P, S], F32, name=f"h{t}")
             for h in range(HALVES):
                 nc.vector.tensor_tensor(hrow[:, half(h)], sums[t, "w1", h][:], bounded[t, h][:], ALU.add)
-            patch_weights((t - 1) % PACK)
-            pages[t] = keep.tile([P, S], F32, name=f"page{t}")
-            nc.scalar.activation(pages[t][:], hrow[:], ACT.Copy, scale=row_vals["skip"][:, col])
+            feats[t] = hrow
             nc.vector.reduce_max(top[:, col], hrow[:], axis=mybir.AxisListType.X)
             if t == 0:
                 nc.vector.tensor_tensor(look_bias[:, col], top[:, col], neg_open[:, col], ALU.mult)
             else:
                 nc.scalar.activation(look_bias[:, col], top[:, col], ACT.Copy, scale=neg_open[:, col])
-            looks[t] = ring.tile([P, PICK], F32, name="look")
+
+        def look(t):
+            col = slice(t, t + 1)
+            looks[t] = keep.tile([P, PICK], F32, name=("bounded2_1", "bounded3_0")[t % 2])
             nc.scalar.activation(
-                looks[t][:], hrow[:].indirect(pos1_sb[:]), ACT.Sigmoid,
+                looks[t][:], feats[t][:].indirect(pos1_sb[:]), ACT.Sigmoid,
                 bias=look_bias[:, col], scale=row_vals["sharp"][:, col],
             )
 
         def patch(t):
+            look(t)
+            pages[t] = keep.tile([P, S], F32, name=("bounded2_0", "bounded3_1", "pw0", "pw1")[t])
+            nc.scalar.activation(pages[t][:], feats[t][:], ACT.Copy, scale=row_vals["skip"][:, t : t + 1])
             nc.vector.tensor_tensor(pages[t][:].indirect(pos2_sb[:]), looks[t][:], pw[t][:], ALU.mult)
-            for h in range(HALVES):
-                nc.scalar.activation(
-                    x_rows[h][:, t, :], pages[t][:, half(h)], ACT.Copy, scale=row_vals["gain"][:, t : t + 1]
-                )
 
+        def whole_sums(t, kind):
+            for h in range(HALVES):
+                for a in range(PASSES):
+                    first_stage_pass(t, a, (kind,), (h,))
+
+        bound(0)
+        bound(1)
         for t in range(PACK):
             if t >= 2:
-                for a in range(PASSES):
-                    first_stage_pass(t, a, ("w4",))
-            bound(t)
-        for t in range(PACK + 1):
-            if t < PACK:
-                if t >= 2:
-                    for a in range(PASSES):
-                        first_stage_pass(t, a, ("w1",))
-                features(t)
-            if t >= 1:
-                patch(t - 1)
+                whole_sums(t, "w1")
+            if 1 <= t < PACK - 1:
+                whole_sums(t + 1, "w4")
+                bound(t + 1)
+            features(t)
+        for t in range(PACK):
+            patch_weights(t)
+        for t in range(PACK):
+            patch(t)
 
-        n_tiles = N // P
-        for h in range(HALVES):
-            grouped = ring.tile([P, BANK * PACK], BF16, name="x_grouped", align_bytes=64)
+        chunks = S // CHUNK
+        x_rows = [keep.tile([P, PACK, CHUNK], BF16, name=f"x_rows{c}") for c in range(chunks)]
+        for t in range(PACK):
+            for c in range(chunks):
+                nc.scalar.activation(
+                    x_rows[c][:, t, :], pages[t][:, c * CHUNK : (c + 1) * CHUNK], ACT.Copy,
+                    scale=row_vals["gain"][:, t : t + 1],
+                )
+        pairs = N // (2 * P)
+        for c in range(chunks):
+            grouped = keep.tile([P, CHUNK * PACK], BF16, name=f"x_grouped{c}", align_bytes=64)
             nc.vector.tensor_copy(
                 grouped[:].rearrange("p (c i t) -> p c t i", i=4, t=PACK),
-                x_rows[h][:].rearrange("p t (c i) -> p c t i", i=4),
+                x_rows[c][:].rearrange("p t (c i) -> p c t i", i=4),
             )
-            x_q = keep.tile([P, BANK], U32, name=f"x_q{h}", align_bytes=64)
-            x_sc = keep.tile([P, BANK], U8, name=f"x_sc{h}", align_bytes=64)
+            x_q = keep.tile([P, CHUNK], U32, name=f"x_q{c}", align_bytes=64)
+            x_sc = keep.tile([P, CHUNK], U8, name=f"x_sc{c}", align_bytes=64)
             nc.vector.quantize_mx(x_q[:].bitcast(FP8X4), x_sc[:], grouped[:])
-            for n in range(n_tiles):
-                unit = h * n_tiles + n
-                acc = psum.tile([P, BANK], F32, name=f"bank{unit % 8}")
-                cols = slice(n * P, (n + 1) * P)
-                nc.tensor.matmul_mx(
-                    acc[:], lhsT=w8_sb[:, cols].bitcast(FP8X4), lhsT_scale=w8_sc[:, cols],
-                    rhs=x_q[:].bitcast(FP8X4), rhs_scale=x_sc[:], start=True, stop=True,
-                )
-                staged = keep.tile([P, BANK], F32, name=f"staged{unit % 8}")
-                if h == 0 or n % 3 == 2:
+            for pair in range(pairs):
+                unit = c * pairs + pair
+                acc = psum.tile([P, 2, CHUNK], F32, name=f"bank{unit % 8}")
+                for u in range(2):
+                    cols = slice((2 * pair + u) * P, (2 * pair + u + 1) * P)
+                    nc.tensor.matmul_mx(
+                        acc[:, u, :], lhsT=w8_sb[:, cols].bitcast(FP8X4), lhsT_scale=w8_sc[:, cols],
+                        rhs=x_q[:].bitcast(FP8X4), rhs_scale=x_sc[:], start=True, stop=True,
+                    )
+                staged = keep.tile([P, 2, CHUNK], F32, name=f"staged{unit}")
+                if c < 2 or unit % 2 == 1:
                     nc.scalar.copy(staged[:], acc[:])
                 else:
                     nc.vector.tensor_copy(staged[:], acc[:])
-                nc.sync.dma_start(out[cols, half(h)], staged[:])
+                nc.sync.dma_start(
+                    out[2 * pair * P : 2 * (pair + 1) * P, c * CHUNK : (c + 1) * CHUNK].rearrange("(u p) c -> p u c", u=2),
+                    staged[:],
+                )

@@ -22,7 +22,8 @@ PASSES = K // (P * PACK)
 BANK = 512
 HALVES = S // BANK
 QUADS = 4
-CHUNK = 256
+CHUNKS = ((0, 256), (256, 256), (512, 256), (768, 256))
+ROWS_BYTES = PACK * PICK * 4
 
 
 def tile_list_crackle_patch_readout_kernel(
@@ -33,13 +34,13 @@ def tile_list_crackle_patch_readout_kernel(
     with ExitStack() as ctx:
         lists = ctx.enter_context(tc.tile_pool(name="lists", bufs=1))
         keep = ctx.enter_context(tc.tile_pool(name="keep", bufs=1))
-        ring = ctx.enter_context(tc.tile_pool(name="ring", bufs=2))
+        shared = ctx.enter_context(tc.tile_pool(name="shared", bufs=1))
         psum = ctx.enter_context(tc.psum_pool(name="psum", bufs=1))
 
         def half(h):
             return slice(h * BANK, (h + 1) * BANK)
 
-        tab_sc = keep.tile([P, T], U8, name="tab_sc", align_bytes=64)
+        tab_sc = keep.tile([P, T], U8, name="tab_last", align_bytes=64)
         nc.vector.memset(tab_sc[:].bitcast(I32), 0)
         w4_sc_raw = keep.tile([P, PASSES, H], U8, name="w4_sc_raw", align_bytes=64)
         nc.vector.memset(w4_sc_raw[:].rearrange("p a n -> p (a n)").bitcast(I32), 0)
@@ -54,16 +55,19 @@ def tile_list_crackle_patch_readout_kernel(
         tab_sb, w1_raw = {}, {}
 
         def load_tab(a):
-            tab_sb[a] = keep.tile([P, T], I32, name=("tab_sc" if a == PASSES - 1 else f"tab{a}"), align_bytes=64)
+            if a == 1:
+                tab_sb[a] = shared.tile([P, T], I32, name="tab_middle", align_bytes=64, offset=0)
+            else:
+                tab_sb[a] = keep.tile([P, T], I32, name=("tab_first" if a == 0 else "tab_last"), align_bytes=64)
             nc.sync.dma_start(tab_sb[a][:], tab_words[a].rearrange("p t i -> p (t i)").bitcast(I32))
 
         def load_w1(a):
-            w1_raw[a] = keep.tile([P, PACK, H], F32, name=f"rows{a % 2}")
+            w1_raw[a] = keep.tile([P, PACK, H], F32, name=f"w1_raw{a}")
             nc.sync.dma_start(
                 w1_raw[a][:], w1[a * P * PACK : (a + 1) * P * PACK, :].rearrange("(p j) c -> p j c", j=PACK)
             )
 
-        w4_raw = keep.tile([P, PASSES, H // 2], I32, name="rows1")
+        w4_raw = shared.tile([P, PASSES, H // 2], I32, name="w4_raw", align_bytes=64, offset=0)
         nc.sync.dma_start(offs_sb[:], offs)
         load_tab(0)
         nc.sync.dma_start(pos1_sb[:], pos1)
@@ -72,8 +76,8 @@ def tile_list_crackle_patch_readout_kernel(
         nc.sync.dma_start(
             tab_sc[0 : 16 * PASSES, :].bitcast(I32), tab_scales.rearrange("a q n -> q a n").bitcast(I32)
         )
-        load_w1(0)
-        load_tab(1)
+        for a in range(PASSES):
+            load_w1(a)
         for q in range(QUADS):
             nc.sync.dma_start(
                 w4_sc_raw[32 * q : 32 * q + 4, :, :].bitcast(I32),
@@ -106,10 +110,13 @@ def tile_list_crackle_patch_readout_kernel(
                 )
 
         def quantise_w1(a):
-            grouped = keep.tile([P, H * PACK], BF16, name=f"grouped{a % 2}", align_bytes=64)
+            grouped = keep.tile([P, H * PACK], BF16, name=f"grouped{a}", align_bytes=64)
             dst = grouped[:].rearrange("p (t m j) -> p m j t", t=PACK, j=PACK)
             src = w1_raw[a][:].rearrange("p j (m t) -> p m j t", t=PACK)
-            nc.scalar.copy(dst, src)
+            if a == 1:
+                nc.vector.tensor_copy(dst, src)
+            else:
+                nc.scalar.copy(dst, src)
             nc.vector.quantize_mx(w1_q[a][:].bitcast(FP8X4), w1_sc[a][:], grouped[:])
 
         sums = {}
@@ -137,12 +144,12 @@ def tile_list_crackle_patch_readout_kernel(
         w4_sb = keep.tile([P, PASSES, 2 * H], U8, name="w4_sb", align_bytes=64)
         w4_sc = keep.tile([P, PASSES, H], U8, name="w4_sc", align_bytes=64)
         nc.vector.tensor_copy(
-            w4_sb[:].bitcast(U16).rearrange("p a (t m) -> p a m t", t=PACK),
-            w4_raw[:].bitcast(U16).rearrange("p a (m t) -> p a m t", t=PACK),
+            w4_sb[:].bitcast(U16).rearrange("p a (t m) -> p a t m", t=PACK),
+            w4_raw[:].bitcast(U16).rearrange("p a (m t) -> p a t m", t=PACK),
         )
-        load_w1(1)
+        load_tab(1)
         quantise_w1(0)
-        load_w1(2)
+        quantise_w1(1)
         picked_sc = keep.tile([P, S], U8, name="picked_sc", align_bytes=64)
         nc.vector.tensor_copy(picked_sc[:], tab_sc[:].indirect(offs_sb[:]))
         rows = 4 * PASSES
@@ -151,22 +158,23 @@ def tile_list_crackle_patch_readout_kernel(
                 v_sc[32 * q : 32 * q + 4, :].bitcast(I32), picked_sc[rows * q : rows * (q + 1), :].bitcast(I32)
             )
         load_tab(2)
-        gather_pass(1)
         nc.vector.tensor_copy(
-            w4_sc[:].rearrange("p a (t m) -> p a m t", t=PACK),
-            w4_sc_raw[:].rearrange("p a (m t) -> p a m t", t=PACK),
+            w4_sc[:].rearrange("p a (t m) -> p a t m", t=PACK),
+            w4_sc_raw[:].rearrange("p a (m t) -> p a t m", t=PACK),
         )
-        quantise_w1(1)
         quantise_w1(2)
-        pat_sb = keep.tile([P, PACK, PICK], F32, name="rows0")
+        gather_pass(1)
+        pat_sb = shared.tile([P, PACK, PICK], F32, name="pat_sb", align_bytes=64, offset=0)
         nc.sync.dma_start(pat_sb[:], pat.rearrange("(p t) m -> p t m", t=PACK))
-        wgs_sb = keep.tile([P, PACK, PICK], F32, name="grouped0", align_bytes=64)
-        for q in range(QUADS):
-            nc.sync.dma_start(wgs_sb[32 * q : 32 * (q + 1), :, :], wgs.rearrange("(p t) m -> p t m", t=PACK))
+        wgs_sb = shared.tile([P, PACK, PICK], F32, name="wgs_sb", align_bytes=64, offset=ROWS_BYTES)
+        wgs_rows = wgs.rearrange("(p t) m -> p t m", t=PACK)
+        for u in range(2):
+            for q in (0, 2, 1, 3):
+                nc.sync.dma_start(wgs_sb[32 * q : 32 * (q + 1), 2 * u : 2 * u + 2, :], wgs_rows[:, 2 * u : 2 * u + 2, :])
         gather_pass(2)
-        w8_sb = keep.tile([P, N], I32, name="tab_sc", align_bytes=64)
+        w8_sb = keep.tile([P, N], I32, name="tab_last", align_bytes=64)
         nc.sync.dma_start(w8_sb[:], w8_words[0].rearrange("p n i -> p (n i)").bitcast(I32))
-        for kind, a in (("w1", 0), ("w4", 0), ("w4", 1), ("w1", 1)):
+        for kind, a in (("w1", 0), ("w4", 0), ("w1", 1), ("w4", 1)):
             for t in range(2):
                 first_stage_pass(t, a, (kind,), range(HALVES))
         for h in range(HALVES):
@@ -204,7 +212,7 @@ def tile_list_crackle_patch_readout_kernel(
 
         def look(t):
             col = slice(t, t + 1)
-            looks[t] = keep.tile([P, PICK], F32, name=("bounded2_1", "bounded3_0")[t % 2])
+            looks[t] = keep.tile([P, PICK], F32, name=("look0", "bounded2_0")[t % 2])
             nc.scalar.activation(
                 looks[t][:], feats[t][:].indirect(pos1_sb[:]), ACT.Sigmoid,
                 bias=look_bias[:, col], scale=row_vals["sharp"][:, col],
@@ -212,7 +220,7 @@ def tile_list_crackle_patch_readout_kernel(
 
         def patch(t):
             look(t)
-            pages[t] = keep.tile([P, S], F32, name=("bounded2_0", "bounded3_1", "pw0", "pw1")[t])
+            pages[t] = keep.tile([P, S], F32, name=("bounded1_1", "bounded2_1", "pw0", "pw1")[t])
             nc.scalar.activation(pages[t][:], feats[t][:], ACT.Copy, scale=row_vals["skip"][:, t : t + 1])
             nc.vector.tensor_tensor(pages[t][:].indirect(pos2_sb[:]), looks[t][:], pw[t][:], ALU.mult)
 
@@ -221,6 +229,8 @@ def tile_list_crackle_patch_readout_kernel(
                 for a in range(PASSES):
                     first_stage_pass(t, a, (kind,), (h,))
 
+        for t in range(PACK):
+            patch_weights(t)
         bound(0)
         bound(1)
         for t in range(PACK):
@@ -229,45 +239,44 @@ def tile_list_crackle_patch_readout_kernel(
             if 1 <= t < PACK - 1:
                 whole_sums(t + 1, "w4")
                 bound(t + 1)
+            if t == PACK - 1:
+                patch(0)
             features(t)
-        for t in range(PACK):
-            patch_weights(t)
-        for t in range(PACK):
+        for t in range(1, PACK):
             patch(t)
 
-        chunks = S // CHUNK
-        x_rows = [keep.tile([P, PACK, CHUNK], BF16, name=f"x_rows{c}") for c in range(chunks)]
+        x_rows = [keep.tile([P, PACK, width], BF16, name=f"x_rows{c}") for c, (first, width) in enumerate(CHUNKS)]
         for t in range(PACK):
-            for c in range(chunks):
+            for c, (first, width) in enumerate(CHUNKS):
                 nc.scalar.activation(
-                    x_rows[c][:, t, :], pages[t][:, c * CHUNK : (c + 1) * CHUNK], ACT.Copy,
+                    x_rows[c][:, t, :], pages[t][:, first : first + width], ACT.Copy,
                     scale=row_vals["gain"][:, t : t + 1],
                 )
-        pairs = N // (2 * P)
-        for c in range(chunks):
-            grouped = keep.tile([P, CHUNK * PACK], BF16, name=f"x_grouped{c}", align_bytes=64)
+        unit = 0
+        for c, (first, width) in enumerate(CHUNKS):
+            grouped = keep.tile([P, width * PACK], BF16, name=f"x_grouped{c}", align_bytes=64)
             nc.vector.tensor_copy(
                 grouped[:].rearrange("p (c i t) -> p c t i", i=4, t=PACK),
                 x_rows[c][:].rearrange("p t (c i) -> p c t i", i=4),
             )
-            x_q = keep.tile([P, CHUNK], U32, name=f"x_q{c}", align_bytes=64)
-            x_sc = keep.tile([P, CHUNK], U8, name=f"x_sc{c}", align_bytes=64)
+            x_q = keep.tile([P, width], U32, name=f"x_q{c}", align_bytes=64)
+            x_sc = keep.tile([P, width], U8, name=f"x_sc{c}", align_bytes=64)
             nc.vector.quantize_mx(x_q[:].bitcast(FP8X4), x_sc[:], grouped[:])
-            for pair in range(pairs):
-                unit = c * pairs + pair
-                acc = psum.tile([P, 2, CHUNK], F32, name=f"bank{unit % 8}")
-                for u in range(2):
-                    cols = slice((2 * pair + u) * P, (2 * pair + u + 1) * P)
+            side = BANK // width
+            for n0 in range(0, N, side * P):
+                acc = psum.tile([P, side, width], F32, name=f"bank{unit % 8}")
+                for u in range(side):
+                    cols = slice(n0 + u * P, n0 + (u + 1) * P)
                     nc.tensor.matmul_mx(
                         acc[:, u, :], lhsT=w8_sb[:, cols].bitcast(FP8X4), lhsT_scale=w8_sc[:, cols],
                         rhs=x_q[:].bitcast(FP8X4), rhs_scale=x_sc[:], start=True, stop=True,
                     )
-                staged = keep.tile([P, 2, CHUNK], F32, name=f"staged{unit}")
+                staged = keep.tile([P, side, width], F32, name=f"staged{unit}")
                 if c < 2 or unit % 2 == 1:
                     nc.scalar.copy(staged[:], acc[:])
                 else:
                     nc.vector.tensor_copy(staged[:], acc[:])
                 nc.sync.dma_start(
-                    out[2 * pair * P : 2 * (pair + 1) * P, c * CHUNK : (c + 1) * CHUNK].rearrange("(u p) c -> p u c", u=2),
-                    staged[:],
+                    out[n0 : n0 + side * P, first : first + width].rearrange("(u p) c -> p u c", u=side), staged[:]
                 )
+                unit = unit + 1

@@ -22,7 +22,7 @@ PASSES = K // (P * PACK)
 BANK = 512
 HALVES = S // BANK
 QUADS = 4
-CHUNKS = ((0, 256), (256, 256), (512, 256), (768, 256))
+CHUNKS = ((0, 256), (256, 256), (512, 512))
 ROWS_BYTES = PACK * PICK * 4
 
 
@@ -56,28 +56,31 @@ def tile_list_crackle_patch_readout_kernel(
 
         def load_tab(a):
             if a == 1:
-                tab_sb[a] = shared.tile([P, T], I32, name="tab_middle", align_bytes=64, offset=0)
+                tab_sb[a] = shared.tile([P, T], I32, name="tab_middle", align_bytes=64, offset=ROWS_BYTES)
             else:
                 tab_sb[a] = keep.tile([P, T], I32, name=("tab_first" if a == 0 else "tab_last"), align_bytes=64)
             nc.sync.dma_start(tab_sb[a][:], tab_words[a].rearrange("p t i -> p (t i)").bitcast(I32))
 
         def load_w1(a):
-            w1_raw[a] = keep.tile([P, PACK, H], F32, name=f"w1_raw{a}")
+            if a == PASSES - 1:
+                w1_raw[a] = shared.tile([P, PACK, H], F32, name="w1_last", align_bytes=64, offset=0)
+            else:
+                w1_raw[a] = keep.tile([P, PACK, H], F32, name=f"w1_raw{a}")
             nc.sync.dma_start(
                 w1_raw[a][:], w1[a * P * PACK : (a + 1) * P * PACK, :].rearrange("(p j) c -> p j c", j=PACK)
             )
 
-        w4_raw = shared.tile([P, PASSES, H // 2], I32, name="w4_raw", align_bytes=64, offset=0)
-        nc.sync.dma_start(offs_sb[:], offs)
+        w4_raw = shared.tile([P, PASSES, H // 2], I32, name="w4_raw", align_bytes=64, offset=ROWS_BYTES - PASSES * H)
         load_tab(0)
+        nc.sync.dma_start(offs_sb[:], offs)
         nc.sync.dma_start(pos1_sb[:], pos1)
         nc.sync.dma_start(pos2_sb[:], pos2)
         nc.sync.dma_start(w4_raw[:], w4_words.rearrange("a p n -> p a n").bitcast(I32))
         nc.sync.dma_start(
             tab_sc[0 : 16 * PASSES, :].bitcast(I32), tab_scales.rearrange("a q n -> q a n").bitcast(I32)
         )
-        for a in range(PASSES):
-            load_w1(a)
+        load_w1(0)
+        load_w1(1)
         for q in range(QUADS):
             nc.sync.dma_start(
                 w4_sc_raw[32 * q : 32 * q + 4, :, :].bitcast(I32),
@@ -113,7 +116,7 @@ def tile_list_crackle_patch_readout_kernel(
             grouped = keep.tile([P, H * PACK], BF16, name=f"grouped{a}", align_bytes=64)
             dst = grouped[:].rearrange("p (t m j) -> p m j t", t=PACK, j=PACK)
             src = w1_raw[a][:].rearrange("p j (m t) -> p m j t", t=PACK)
-            if a == 1:
+            if a == PASSES - 1:
                 nc.vector.tensor_copy(dst, src)
             else:
                 nc.scalar.copy(dst, src)
@@ -147,9 +150,9 @@ def tile_list_crackle_patch_readout_kernel(
             w4_sb[:].bitcast(U16).rearrange("p a (t m) -> p a t m", t=PACK),
             w4_raw[:].bitcast(U16).rearrange("p a (m t) -> p a t m", t=PACK),
         )
+        load_w1(2)
         load_tab(1)
         quantise_w1(0)
-        quantise_w1(1)
         picked_sc = keep.tile([P, S], U8, name="picked_sc", align_bytes=64)
         nc.vector.tensor_copy(picked_sc[:], tab_sc[:].indirect(offs_sb[:]))
         rows = 4 * PASSES
@@ -162,11 +165,12 @@ def tile_list_crackle_patch_readout_kernel(
             w4_sc[:].rearrange("p a (t m) -> p a t m", t=PACK),
             w4_sc_raw[:].rearrange("p a (m t) -> p a t m", t=PACK),
         )
+        quantise_w1(1)
         quantise_w1(2)
         gather_pass(1)
-        pat_sb = shared.tile([P, PACK, PICK], F32, name="pat_sb", align_bytes=64, offset=0)
+        pat_sb = shared.tile([P, PACK, PICK], F32, name="pat_sb", align_bytes=64, offset=ROWS_BYTES)
         nc.sync.dma_start(pat_sb[:], pat.rearrange("(p t) m -> p t m", t=PACK))
-        wgs_sb = shared.tile([P, PACK, PICK], F32, name="wgs_sb", align_bytes=64, offset=ROWS_BYTES)
+        wgs_sb = shared.tile([P, PACK, PICK], F32, name="wgs_sb", align_bytes=64, offset=2 * ROWS_BYTES)
         wgs_rows = wgs.rearrange("(p t) m -> p t m", t=PACK)
         for u in range(2):
             for q in (0, 2, 1, 3):

from contextlib import ExitStack

import concourse.mybir as mybir

K, H, N, T, S, PICK = 1536, 512, 768, 4096, 1024, 512
FLOPS = 2 * (2 * K * H * S + H * N * S)

F32 = mybir.dt.float32
BF16 = mybir.dt.bfloat16
I32 = mybir.dt.int32
U32 = mybir.dt.uint32
U16 = mybir.dt.uint16
U8 = mybir.dt.uint8
FP8X4 = mybir.dt.float8_e4m3fn_x4
FP4X4 = mybir.dt.float4_e2m1fn_x4
ACT = mybir.ActivationFunctionType
ALU = mybir.AluOpType

P = 128
PACK = 4
PASSES = K // (P * PACK)
BANK = 512
HALVES = S // BANK
QUADS = 4
CHUNKS = ((0, 256), (256, 256), (512, 512))
ROWS_BYTES = PACK * PICK * 4


def tile_list_crackle_patch_readout_kernel(
    tc, tab_words, tab_scales, offs, pos1, pos2, w1, w4_words, w4_scales, b4, sharp, share, pat, skip, wgs, gain,
    w8_words, w8_scales, out,
):
    nc = tc.nc
    with ExitStack() as ctx:
        lists = ctx.enter_context(tc.tile_pool(name="lists", bufs=1))
        keep = ctx.enter_context(tc.tile_pool(name="keep", bufs=1))
        shared = ctx.enter_context(tc.tile_pool(name="shared", bufs=1))
        psum = ctx.enter_context(tc.psum_pool(name="psum", bufs=1))

        def half(h):
            return slice(h * BANK, (h + 1) * BANK)

        tab_sc = keep.tile([P, T], U8, name="tab_last", align_bytes=64)
        nc.vector.memset(tab_sc[:].bitcast(I32), 0)
        w4_sc_raw = keep.tile([P, PASSES, H], U8, name="w4_sc_raw", align_bytes=64)
        nc.vector.memset(w4_sc_raw[:].rearrange("p a n -> p (a n)").bitcast(I32), 0)
        v_sc = keep.tile([P, PASSES * S], U8, name="v_sc", align_bytes=64)
        nc.vector.memset(v_sc[:].bitcast(I32), 0)
        w8_sc = keep.tile([P, N], U8, name="w8_sc", align_bytes=64)
        nc.vector.memset(w8_sc[:].bitcast(I32), 0)

        offs_sb = lists.tile([P, S // 16], U16, name="offs_sb")
        pos1_sb = lists.tile([P, PICK // 16], U16, name="pos1_sb")
        pos2_sb = lists.tile([P, PICK // 16], U16, name="pos2_sb")
        tab_sb, w1_raw = {}, {}

        def load_tab(a):
            if a == 1:
                tab_sb[a] = shared.tile([P, T], I32, name="tab_middle", align_bytes=64, offset=ROWS_BYTES)
            else:
                tab_sb[a] = keep.tile([P, T], I32, name=("tab_first" if a == 0 else "tab_last"), align_bytes=64)
            nc.sync.dma_start(tab_sb[a][:], tab_words[a].rearrange("p t i -> p (t i)").bitcast(I32))

        def load_w1(a):
            if a == PASSES - 1:
                w1_raw[a] = shared.tile([P, PACK, H], F32, name="w1_last", align_bytes=64, offset=0)
            else:
                w1_raw[a] = keep.tile([P, PACK, H], F32, name=f"w1_raw{a}")
            nc.sync.dma_start(
                w1_raw[a][:], w1[a * P * PACK : (a + 1) * P * PACK, :].rearrange("(p j) c -> p j c", j=PACK)
            )

        w4_raw = shared.tile([P, PASSES, H // 2], I32, name="w4_raw", align_bytes=64, offset=ROWS_BYTES - PASSES * H)
        load_tab(0)
        nc.sync.dma_start(offs_sb[:], offs)
        nc.sync.dma_start(pos1_sb[:], pos1)
        nc.sync.dma_start(pos2_sb[:], pos2)
        nc.sync.dma_start(w4_raw[:], w4_words.rearrange("a p n -> p a n").bitcast(I32))
        nc.sync.dma_start(
            tab_sc[0 : 16 * PASSES, :].bitcast(I32), tab_scales.rearrange("a q n -> q a n").bitcast(I32)
        )
        load_w1(0)
        load_w1(1)
        for q in range(QUADS):
            nc.sync.dma_start(
                w4_sc_raw[32 * q : 32 * q + 4, :, :].bitcast(I32),
                w4_scales[:, 4 * q : 4 * q + 4, :].rearrange("a r n -> r a n").bitcast(I32),
            )

        row_vals = {}
        for name, vec in (("b4", b4), ("sharp", sharp), ("share", share), ("skip", skip), ("gain", gain)):
            row_vals[name] = keep.tile([P, PACK], F32, name=f"{name}_sb")
            nc.gpsimd.dma_start(row_vals[name][:], vec.rearrange("(p t) -> p t", t=PACK))
        for q in range(QUADS):
            nc.gpsimd.dma_start(
                w8_sc[32 * q : 32 * q + 4, :].bitcast(I32), w8_scales[0, 4 * q : 4 * q + 4, :].bitcast(I32)
            )

        neg_open = keep.tile([P, PACK], F32, name="neg_open")
        opening = keep.tile([P, PACK], F32, name="opening")
        nc.gpsimd.tensor_tensor(opening[:], row_vals["sharp"][:], row_vals["share"][:], ALU.mult)
        nc.gpsimd.tensor_scalar(neg_open[:], opening[:], -1.0, 0.0, ALU.mult, ALU.add)

        v_words = [[keep.tile([P, BANK], U32, name=f"v{a}_{h}", align_bytes=64) for h in range(HALVES)] for a in range(PASSES)]
        w1_q = [keep.tile([P, H], U32, name=f"w1_q{a}", align_bytes=64) for a in range(PASSES)]
        w1_sc = [keep.tile([P, H], U8, name=f"w1_sc{a}", align_bytes=64) for a in range(PASSES)]

        def gather_pass(a):
            cols = BANK // 16
            for h in range(HALVES):
                nc.vector.tensor_copy(
                    v_words[a][h][:], tab_sb[a][:].bitcast(U32).indirect(offs_sb[:, h * cols : (h + 1) * cols])
                )

        def quantise_w1(a):
            grouped = keep.tile([P, H * PACK], BF16, name=f"grouped{a}", align_bytes=64)
            dst = grouped[:].rearrange("p (t m j) -> p m j t", t=PACK, j=PACK)
            src = w1_raw[a][:].rearrange("p j (m t) -> p m j t", t=PACK)
            if a == PASSES - 1:
                nc.vector.tensor_copy(dst, src)
            else:
                nc.scalar.copy(dst, src)
            nc.vector.quantize_mx(w1_q[a][:].bitcast(FP8X4), w1_sc[a][:], grouped[:])

        sums = {}

        def first_stage_pass(t, a, kinds, halves):
            m = slice(t * P, (t + 1) * P)
            for kind in kinds:
                for h in halves:
                    if a == 0:
                        bank = 4 * (t % 2) + 2 * (kind == "w1") + h
                        sums[t, kind, h] = psum.tile([P, BANK], F32, name=f"bank{bank}")
                    if kind == "w4":
                        lhs = w4_sb[:, a, 2 * t * P : 2 * (t + 1) * P].bitcast(FP4X4)
                        lhs_sc = w4_sc[:, a, m]
                    else:
                        lhs = w1_q[a][:, m].bitcast(FP8X4)
                        lhs_sc = w1_sc[a][:, m]
                    nc.tensor.matmul_mx(
                        sums[t, kind, h][:], lhsT=lhs, lhsT_scale=lhs_sc,
                        rhs=v_words[a][h][:].bitcast(FP8X4), rhs_scale=v_sc[:, a * S + h * BANK : a * S + (h + 1) * BANK],
                        start=(a == 0), stop=(a == PASSES - 1),
                    )

        gather_pass(0)
        w4_sb = keep.tile([P, PASSES, 2 * H], U8, name="w4_sb", align_bytes=64)
        w4_sc = keep.tile([P, PASSES, H], U8, name="w4_sc", align_bytes=64)
        nc.vector.tensor_copy(
            w4_sb[:].bitcast(U16).rearrange("p a (t m) -> p a t m", t=PACK),
            w4_raw[:].bitcast(U16).rearrange("p a (m t) -> p a t m", t=PACK),
        )
        load_w1(2)
        load_tab(1)
        quantise_w1(0)
        picked_sc = keep.tile([P, S], U8, name="picked_sc", align_bytes=64)
        nc.vector.tensor_copy(picked_sc[:], tab_sc[:].indirect(offs_sb[:]))
        rows = 4 * PASSES
        for q in range(QUADS):
            nc.sync.dma_start(
                v_sc[32 * q : 32 * q + 4, :].bitcast(I32), picked_sc[rows * q : rows * (q + 1), :].bitcast(I32)
            )
        load_tab(2)
        nc.vector.tensor_copy(
            w4_sc[:].rearrange("p a (t m) -> p a t m", t=PACK),
            w4_sc_raw[:].rearrange("p a (m t) -> p a t m", t=PACK),
        )
        quantise_w1(1)
        quantise_w1(2)
        gather_pass(1)
        pat_sb = shared.tile([P, PACK, PICK], F32, name="pat_sb", align_bytes=64, offset=ROWS_BYTES)
        nc.sync.dma_start(pat_sb[:], pat.rearrange("(p t) m -> p t m", t=PACK))
        wgs_sb = shared.tile([P, PACK, PICK], F32, name="wgs_sb", align_bytes=64, offset=2 * ROWS_BYTES)
        wgs_rows = wgs.rearrange("(p t) m -> p t m", t=PACK)
        for u in range(2):
            for q in (0, 2, 1, 3):
                nc.sync.dma_start(wgs_sb[32 * q : 32 * (q + 1), 2 * u : 2 * u + 2, :], wgs_rows[:, 2 * u : 2 * u + 2, :])
        gather_pass(2)
        w8_sb = keep.tile([P, N], I32, name="tab_last", align_bytes=64)
        nc.sync.dma_start(w8_sb[:], w8_words[0].rearrange("p n i -> p (n i)").bitcast(I32))
        for kind, a in (("w1", 0), ("w4", 0), ("w1", 1), ("w4", 1)):
            for t in range(2):
                first_stage_pass(t, a, (kind,), range(HALVES))
        for h in range(HALVES):
            for t in range(2):
                first_stage_pass(t, PASSES - 1, ("w4", "w1"), (h,))

        pw, bounded = {}, {}

        def bound(t):
            for h in range(HALVES):
                bounded[t, h] = keep.tile([P, BANK], F32, name=f"bounded{t}_{h}")
                nc.scalar.activation(
                    bounded[t, h][:], sums[t, "w4", h][:], ACT.Tanh, bias=row_vals["b4"][:, t : t + 1]
                )

        def patch_weights(t):
            pw[t] = keep.tile([P, PICK], F32, name=f"pw{t}")
            nc.gpsimd.tensor_tensor(pw[t][:], pat_sb[:, t, :], wgs_sb[:, t, :], ALU.mult)

        top = keep.tile([P, PACK], F32, name="top")
        look_bias = keep.tile([P, PACK], F32, name="look_bias")
        pages, looks, feats = {}, {}, {}

        def features(t):
            col = slice(t, t + 1)
            hrow = keep.tile([P, S], F32, name=f"h{t}")
            for h in range(HALVES):
                nc.vector.tensor_tensor(hrow[:, half(h)], sums[t, "w1", h][:], bounded[t, h][:], ALU.add)
            feats[t] = hrow
            nc.vector.reduce_max(top[:, col], hrow[:], axis=mybir.AxisListType.X)
            if t == 0:
                nc.vector.tensor_tensor(look_bias[:, col], top[:, col], neg_open[:, col], ALU.mult)
            else:
                nc.scalar.activation(look_bias[:, col], top[:, col], ACT.Copy, scale=neg_open[:, col])

        def look(t):
            col = slice(t, t + 1)
            looks[t] = keep.tile([P, PICK], F32, name=("look0", "bounded2_0")[t % 2])
            nc.scalar.activation(
                looks[t][:], feats[t][:].indirect(pos1_sb[:]), ACT.Sigmoid,
                bias=look_bias[:, col], scale=row_vals["sharp"][:, col],
            )

        def patch(t):
            look(t)
            pages[t] = keep.tile([P, S], F32, name=("bounded1_1", "bounded2_1", "pw0", "pw1")[t])
            nc.scalar.activation(pages[t][:], feats[t][:], ACT.Copy, scale=row_vals["skip"][:, t : t + 1])
            nc.vector.tensor_tensor(pages[t][:].indirect(pos2_sb[:]), looks[t][:], pw[t][:], ALU.mult)

        def whole_sums(t, kind):
            for h in range(HALVES):
                for a in range(PASSES):
                    first_stage_pass(t, a, (kind,), (h,))

        for t in range(PACK):
            patch_weights(t)
        bound(0)
        bound(1)
        for t in range(PACK):
            if t >= 2:
                whole_sums(t, "w1")
            if 1 <= t < PACK - 1:
                whole_sums(t + 1, "w4")
                bound(t + 1)
            if t == PACK - 1:
                patch(0)
            features(t)
        for t in range(1, PACK):
            patch(t)

        x_rows = [keep.tile([P, PACK, width], BF16, name=f"x_rows{c}") for c, (first, width) in enumerate(CHUNKS)]
        for t in range(PACK):
            for c, (first, width) in enumerate(CHUNKS):
                nc.scalar.activation(
                    x_rows[c][:, t, :], pages[t][:, first : first + width], ACT.Copy,
                    scale=row_vals["gain"][:, t : t + 1],
                )
        unit = 0
        for c, (first, width) in enumerate(CHUNKS):
            grouped = keep.tile([P, width * PACK], BF16, name=f"x_grouped{c}", align_bytes=64)
            nc.vector.tensor_copy(
                grouped[:].rearrange("p (c i t) -> p c t i", i=4, t=PACK),
                x_rows[c][:].rearrange("p t (c i) -> p c t i", i=4),
            )
            x_q = keep.tile([P, width], U32, name=f"x_q{c}", align_bytes=64)
            x_sc = keep.tile([P, width], U8, name=f"x_sc{c}", align_bytes=64)
            nc.vector.quantize_mx(x_q[:].bitcast(FP8X4), x_sc[:], grouped[:])
            side = BANK // width
            for n0 in range(0, N, side * P):
                acc = psum.tile([P, side, width], F32, name=f"bank{unit % 8}")
                for u in range(side):
                    cols = slice(n0 + u * P, n0 + (u + 1) * P)
                    nc.tensor.matmul_mx(
                        acc[:, u, :], lhsT=w8_sb[:, cols].bitcast(FP8X4), lhsT_scale=w8_sc[:, cols],
                        rhs=x_q[:].bitcast(FP8X4), rhs_scale=x_sc[:], start=True, stop=True,
                    )
                staged = keep.tile([P, side, width], F32, name=f"staged{unit}")
                if c < 2 or unit % 2 == 1:
                    nc.scalar.copy(staged[:], acc[:])
                else:
                    nc.vector.tensor_copy(staged[:], acc[:])
                nc.sync.dma_start(
                    out[n0 : n0 + side * P, first : first + width].rearrange("(u p) c -> p u c", u=side), staged[:]
                )
                unit = unit + 1
